import numpy as np
import ml_dtypes


def mxq(x, axis, fmt="e4m3"):
    dtype, down = {"e4m3": (ml_dtypes.float8_e4m3fn, 7), "e5m2": (ml_dtypes.float8_e5m2, 14)}[fmt]
    v = np.moveaxis(np.asarray(x, np.float32).astype(ml_dtypes.bfloat16).astype(np.float64), axis, -1)
    blocks = v.reshape(v.shape[:-1] + (-1, 32))
    amax = np.abs(blocks).max(-1, keepdims=True)
    byte = np.maximum(np.where(amax > 0, np.frexp(amax)[1] - 1 + 127, 0) - down, 1)
    scale = np.exp2(byte - 127.0)
    codes = (blocks / scale).astype(np.float32).astype(dtype).astype(np.float64)
    return np.moveaxis((codes * scale).reshape(v.shape), -1, axis)


WIDE = False


def mx_kscale(k):
    if not WIDE:
        return np.ones(k)
    levels = np.array([10, -10, 5, -5, 0])
    if k % 512:
        return np.exp2(np.random.permutation(np.resize(levels, k // 32))).repeat(32)
    a = np.empty((k // 512, 16))
    for p in range(k // 512):
        a[p, :8] = np.random.permutation(np.resize(levels, 8))
        for g in range(8):
            far = levels[np.abs(levels - a[p, g]) >= 10]
            a[p, g + 8] = far[np.random.randint(len(far))]
    return np.exp2(a.ravel()).repeat(32)


def f64(x):
    return np.asarray(x).astype(np.float64)


def striped(idx):
    return np.tile(idx.reshape(-1, 16).T, (8, 1)).astype(np.uint16)


def unstriped(offs):
    return offs[:16].T.reshape(-1).astype(np.int64)


E2M1 = np.array([0.0, 0.5, 1.0, 1.5, 2.0, 3.0, 4.0, 6.0, -0.0, -0.5, -1.0, -1.5, -2.0, -3.0, -4.0, -6.0])


def pack_weight(w, fmt):
    k, n = w.shape
    w = f64(np.asarray(w, np.float32).astype(ml_dtypes.bfloat16)).reshape(k // 32, 32, n)
    amax = np.abs(w).max(1)
    if fmt == "e4m3":
        byte = np.frexp(amax)[1] - 1 + 127 - 7
    else:
        mant, ex = np.frexp(amax / 6.0)
        byte = np.where(mant > 0.5, ex, ex - 1) + 127
    byte = np.clip(np.where(amax > 0, byte, 1), 1, 254)
    scaled = (w * np.exp2(127.0 - byte)[:, None, :]).reshape(k, n).astype(np.float32)
    by_word = np.ascontiguousarray(scaled.reshape(k // 512, 128, 4, n).transpose(0, 1, 3, 2))
    if fmt == "e4m3":
        words = by_word.astype(ml_dtypes.float8_e4m3fn).view(np.uint8)
    else:
        c = by_word.astype(ml_dtypes.float4_e2m1fn).view(np.uint8) & 0xF
        words = (c[..., 0::2] | (c[..., 1::2] << 4)).reshape(k // 512, 128, 2 * n)
    return np.ascontiguousarray(words), np.ascontiguousarray(byte.astype(np.uint8).reshape(k // 512, 16, n))


def unpack_weight(words, scales, fmt):
    g, _, n = scales.shape
    words = np.ascontiguousarray(words).reshape(g, 128, n, -1)
    if fmt == "e4m3":
        vals = words.view(ml_dtypes.float8_e4m3fn).astype(np.float64)
    else:
        nib = np.empty((g, 128, n, 4), np.uint8)
        nib[..., 0::2] = words & 0xF
        nib[..., 1::2] = words >> 4
        vals = E2M1[nib]
    vals = vals * np.repeat(np.exp2(scales.astype(np.float64) - 127.0), 8, axis=1)[..., None]
    return vals.transpose(0, 1, 3, 2).reshape(g * 512, n)


def gelu(v):
    return 0.5 * v * (1.0 + np.tanh(np.sqrt(2.0 / np.pi) * (v + 0.044715 * v**3)))


K, T, S, P, H, N = 1536, 2048, 1024, 512, 512, 768


def setup_inputs():
    n = np.random.standard_normal
    s = mx_kscale(K)[:, None]
    u = mx_kscale(H)[:, None]
    tab_words, tab_scales = pack_weight(n((K, T)) * s, "e4m3")
    w4_words, w4_scales = pack_weight(n((H, N)) / np.sqrt(H) / u, "e2m1")
    phase = np.random.choice([-1.0, 1.0], H) * np.random.uniform(0.4, 1.35, H)
    return {
        "tab_words": tab_words, "tab_scales": tab_scales,
        "offs": striped(np.random.permutation(T)[:S]),
        "pos1": striped(np.random.permutation(S)[:P]),
        "pos2": striped(np.random.permutation(S)[:P]),
        "w1": (0.34 * n((K, H)) / np.sqrt(K) / s).astype(np.float32),
        "phase": phase.astype(np.float32),
        "cal": np.random.uniform(0.6, 3.0, H).astype(np.float32),
        "calb": n(H).astype(np.float32),
        "thr": n(H).astype(np.float32),
        "pairs": (3.0 * n((H, P)) * u).astype(np.float32),
        "w4_words": w4_words, "w4_scales": w4_scales,
        "reader": np.exp(0.5 * n(N)).astype(np.float32),
    }


def reference(tab_words, tab_scales, offs, pos1, pos2, w1, phase, cal, calb, thr, pairs, w4_words, w4_scales, reader):
    v = unpack_weight(tab_words, tab_scales, "e4m3")[:, unstriped(offs)]
    h = np.sin((mxq(f64(w1), 0, "e4m3").T @ v) + f64(phase)[:, None])
    a = 1.0 / (1.0 + np.exp(-(f64(cal)[:, None] * h[:, unstriped(pos1)] + f64(calb)[:, None])))
    c = 1.0 / (1.0 + np.exp(-(h[:, unstriped(pos2)] + f64(thr)[:, None])))
    y = mxq(a * c * f64(pairs), 0, "e4m3")
    w4 = unpack_weight(w4_words, w4_scales, "e2m1")
    return f64(reader)[:, None] * (w4.T @ y)

@@ -1,0 +1,257 @@
+from contextlib import ExitStack
+
+import concourse.mybir as mybir
+
+K, T, S, M, H, N = 1536, 2048, 1024, 512, 512, 768
+FLOPS = 2 * K * H * S + 2 * H * N * M
+
+F32 = mybir.dt.float32
+BF16 = mybir.dt.bfloat16
+I32 = mybir.dt.int32
+U32 = mybir.dt.uint32
+U16 = mybir.dt.uint16
+U8 = mybir.dt.uint8
+FP8X4 = mybir.dt.float8_e4m3fn_x4
+FP4X4 = mybir.dt.float4_e2m1fn_x4
+ACT = mybir.ActivationFunctionType
+ALU = mybir.AluOpType
+
+P = 128
+PACK = 4
+PASSES = K // (P * PACK)
+BANK = 512
+HALVES = S // BANK
+PIECE = 256
+PIECES = M // PIECE
+BLOCKS = N // P
+QUADS = 4
+
+
+def tile_list_framework_uptake_screen_kernel(
+    tc, tab_words, tab_scales, offs, pos1, pos2, w1, phase, cal, calb, thr, pairs, w4_words, w4_scales, reader, out
+):
+    nc = tc.nc
+    with ExitStack() as ctx:
+        sb = ctx.enter_context(tc.tile_pool(name="sb", bufs=1))
+        psum = ctx.enter_context(tc.psum_pool(name="psum", bufs=1))
+
+        def tile(name, shape, dtype, tag=None):
+            return sb.tile(shape, dtype, name=name, tag=tag or name, align_bytes=64)
+
+        def bank(index):
+            return psum.tile([P, BANK], F32, name="bank%d" % index, tag="bank%d" % index)
+
+        offs_sb = tile("offs_sb", [P, S // 16], U16)
+        pos1_sb = tile("pos1_sb", [P, M // 16], U16)
+        pos2_sb = tile("pos2_sb", [P, M // 16], U16)
+        tab_sb = [tile("tab%d" % a, [P, T], I32) for a in range(PASSES)]
+        w1_sb = [tile("w1_%d" % a, [P, PACK, H], F32) for a in range(PASSES)]
+        tab_planes = tile("tab_planes", [P, T], U8)
+        w4_plane = tile("w4_plane", [P, N], U8)
+        w4_sb = tile("w4_sb", [P, 2 * N], U8)
+        pairs_sb = tile("pairs_sb", [P, PACK, M], F32)
+        phase_sb = tile("phase_sb", [P, PACK], F32)
+        cal_sb = tile("cal_sb", [P, PACK], F32)
+        calb_sb = tile("calb_sb", [P, PACK], F32)
+        thr_sb = tile("thr_sb", [P, PACK], F32)
+        reader_sb = tile("reader_sb", [P, BLOCKS], F32)
+
+        nc.gpsimd.memset(tab_planes[:].bitcast(I32), 0)
+        nc.vector.memset(w4_plane[:].bitcast(I32), 0)
+        for q in range(QUADS):
+            nc.scalar.dma_start(
+                out=tab_planes[32 * q : 32 * q + 4 * PASSES, :].bitcast(I32),
+                in_=tab_scales[:, 4 * q : 4 * q + 4, :].bitcast(I32),
+            )
+
+        def load_tab(a):
+            nc.sync.dma_start(out=tab_sb[a][:], in_=tab_words[a].rearrange("p n i -> p (n i)").bitcast(I32))
+
+        def load_w1(a):
+            rows = w1[a * P * PACK : (a + 1) * P * PACK, :]
+            nc.sync.dma_start(out=w1_sb[a][:], in_=rows.rearrange("(p i) c -> p i c", i=PACK))
+
+        def load_rows(dst, vec):
+            nc.sync.dma_start(out=dst[:], in_=vec.rearrange("(p t) -> p t", t=PACK))
+
+        load_tab(0)
+        nc.sync.dma_start(offs_sb[:], offs)
+        load_w1(0)
+        load_rows(phase_sb, phase)
+        load_tab(1)
+        load_w1(1)
+        load_w1(2)
+        load_tab(2)
+        nc.sync.dma_start(pos1_sb[:], pos1)
+        load_rows(cal_sb, cal)
+        load_rows(calb_sb, calb)
+        nc.sync.dma_start(out=pairs_sb[:], in_=pairs.rearrange("(p t) m -> p t m", t=PACK))
+        nc.sync.dma_start(pos2_sb[:], pos2)
+        load_rows(thr_sb, thr)
+        nc.sync.dma_start(out=w4_sb[:].bitcast(I32), in_=w4_words[0].bitcast(I32))
+        for q in range(QUADS):
+            nc.sync.dma_start(
+                out=w4_plane[32 * q : 32 * q + 4, :].bitcast(I32),
+                in_=w4_scales[0, 4 * q : 4 * q + 4, :].bitcast(I32),
+            )
+        with nc.allow_non_contiguous_dma(reason="one value of reader for each output row"):
+            nc.sync.dma_start(out=reader_sb[:], in_=reader.rearrange("(b p) -> p b", p=P))
+
+        sin_bias = tile("sin_bias", [P, PACK], F32)
+        nc.vector.tensor_scalar(sin_bias[:], phase_sb[:], -1.0 / 3.0, None, ALU.mult)
+
+        cols = BANK // 16
+
+        def gather_words(a, hf):
+            got = tile("v%d_%d" % (a, hf), [P, BANK], U32)
+            nc.vector.tensor_copy(got[:], tab_sb[a][:].bitcast(U32).indirect(offs_sb[:, hf * cols : (hf + 1) * cols]))
+            return got
+
+        def gather_planes(hf):
+            got = tile("vs%d" % hf, [P, BANK], U8)
+            nc.vector.tensor_copy(got[:], tab_planes[:].indirect(offs_sb[:, hf * cols : (hf + 1) * cols]))
+            return got
+
+        def round_w1(a, u, on_vector):
+            dst = tile("w1b%d_%d" % (a, u), [P, 2 * P * PACK], BF16)
+            dst_view = dst[:].rearrange("p (t m i) -> p m i t", t=2, i=PACK)
+            src_view = w1_sb[a][:].rearrange("p i (m t) -> p m i t", t=PACK)[:, :, :, 2 * u : 2 * u + 2]
+            if on_vector:
+                nc.vector.tensor_copy(dst_view, src_view)
+            else:
+                nc.scalar.copy(dst_view, src_view)
+            return dst
+
+        def quantize(name, src, width):
+            codes = tile(name + "_codes", [P, width], U32)
+            plane = tile(name + "_plane", [P, width], U8)
+            nc.vector.quantize_mx(out=codes[:].bitcast(FP8X4), scales=plane[:], in_=src[:])
+            return codes, plane
+
+        v = {}
+        wq = {}
+        v[0, 0] = gather_words(0, 0)
+        v[0, 1] = gather_words(0, 1)
+        vs = [gather_planes(hf) for hf in range(HALVES)]
+        wb0 = [round_w1(0, u, False) for u in range(2)]
+        v[1, 0] = gather_words(1, 0)
+        for u in range(2):
+            wq[0, u] = quantize("w1q0_%d" % u, wb0[u], 2 * P)
+        v[1, 1] = gather_words(1, 1)
+        for a in (1, 2):
+            wb = [round_w1(a, 0, True), round_w1(a, 1, False)]
+            for u in range(2):
+                wq[a, u] = quantize("w1q%d_%d" % (a, u), wb[u], 2 * P)
+        v[2, 0] = gather_words(2, 0)
+        v[2, 1] = gather_words(2, 1)
+
+        acc = {(t, hf): bank(HALVES * t + hf) for t in range(PACK) for hf in range(HALVES)}
+        for a in range(PASSES):
+            for hf in range(HALVES):
+                for t in range(PACK):
+                    codes, plane = wq[a, t // 2]
+                    lo = (t % 2) * P
+                    nc.tensor.matmul_mx(
+                        out=acc[t, hf][:],
+                        lhsT=codes[:, lo : lo + P].bitcast(FP8X4),
+                        lhsT_scale=plane[:, lo : lo + P],
+                        rhs=v[a, hf][:].bitcast(FP8X4),
+                        rhs_scale=vs[hf][4 * a : P, :],
+                        start=(a == 0),
+                        stop=(a == PASSES - 1),
+                    )
+
+        order = [(0, 0), (1, 0), (0, 1), (1, 1), (2, 0), (2, 1), (3, 0), (3, 1)]
+        h = [tile("h%d" % t, [P, S], F32) for t in range(PACK)]
+        third = [tile("third%d" % t, [P, S], F32) for t in range(PACK)]
+        s = {}
+        for t, hf in order:
+            s[t, hf] = third[t][:, hf * BANK : (hf + 1) * BANK]
+            nc.scalar.activation(s[t, hf], acc[t, hf][:], ACT.Sin, bias=sin_bias[:, t : t + 1], scale=-1.0 / 3.0)
+        sq = {}
+        for first in range(0, len(order), 2):
+            both = order[first : first + 2]
+            for t, hf in both:
+                sq[t, hf] = tile("sq%d_%d" % (t, hf), [P, BANK], F32)
+                nc.vector.scalar_tensor_tensor(sq[t, hf][:], s[t, hf], 4.0, s[t, hf], ALU.mult, ALU.mult)
+            for t, hf in both:
+                nc.vector.scalar_tensor_tensor(
+                    h[t][:, hf * BANK : (hf + 1) * BANK], sq[t, hf][:], 3.0, s[t, hf], ALU.subtract, ALU.mult
+                )
+
+        gate = [tile("gate%d" % t, [P, M], F32) for t in range(PACK)]
+        pcols = PIECE // 16
+        thresh = [
+            tile("thresh0", [P, PACK, PIECE], F32),
+            tile("thresh1", [P, PACK, PIECE], F32, tag="third%d" % (PACK - 1)),
+        ]
+
+        def look_thresh(j, t):
+            nc.scalar.activation(
+                thresh[j][:, t, :],
+                h[t][:].indirect(pos2_sb[:, j * pcols : (j + 1) * pcols]),
+                ACT.Sigmoid,
+                bias=thr_sb[:, t : t + 1],
+            )
+
+        for t in range(PACK):
+            nc.scalar.activation(
+                gate[t][:],
+                h[t][:].indirect(pos1_sb[:]),
+                ACT.Sigmoid,
+                bias=calb_sb[:, t : t + 1],
+                scale=cal_sb[:, t : t + 1],
+            )
+            look_thresh(0, t)
+        for t in range(PACK):
+            look_thresh(1, t)
+
+        weighted = tile("weighted", [P, PACK, M], F32)
+        for t in range(PACK):
+            nc.vector.tensor_tensor(weighted[:, t, :], gate[t][:], pairs_sb[:, t, :], ALU.mult)
+
+        yq = []
+        for j in range(PIECES):
+            y = tile("y%d" % j, [P, PIECE * PACK], BF16, tag="y")
+            nc.vector.tensor_tensor(
+                y[:].rearrange("p (g i t) -> p g t i", i=4, t=PACK),
+                weighted[:, :, j * PIECE : (j + 1) * PIECE].rearrange("p t (g i) -> p g t i", i=4),
+                thresh[j][:].rearrange("p t (g i) -> p g t i", i=4),
+                ALU.mult,
+            )
+            yq.append(quantize("yq%d" % j, y, PIECE))
+
+        out_view = out.rearrange("(b p) m -> p b m", p=P)
+
+        def second(j, b, dst):
+            codes, plane = yq[j]
+            nc.tensor.matmul_mx(
+                out=dst,
+                lhsT=w4_sb[:, 2 * P * b : 2 * P * (b + 1)].bitcast(FP4X4),
+                lhsT_scale=w4_plane[:, P * b : P * (b + 1)],
+                rhs=codes[:].bitcast(FP8X4),
+                rhs_scale=plane[:],
+                start=True,
+                stop=True,
+            )
+
+        for pair in range(BLOCKS // 2):
+            res = bank(pair)
+            staged = tile("first%d" % pair, [P, 2, PIECE], F32)
+            for i in range(2):
+                second(0, 2 * pair + i, res[:, i * PIECE : (i + 1) * PIECE])
+            for i in range(2):
+                b = 2 * pair + i
+                nc.scalar.activation(
+                    staged[:, i, :], res[:, i * PIECE : (i + 1) * PIECE], ACT.Copy, scale=reader_sb[:, b : b + 1]
+                )
+            nc.sync.dma_start(out=out_view[:, 2 * pair : 2 * pair + 2, 0:PIECE], in_=staged[:])
+        for b in range(BLOCKS):
+            res = bank((BLOCKS // 2 + b) % 8)
+            staged = tile("last%d" % b, [P, PIECE], F32)
+            second(1, b, res[:, 0:PIECE])
+            if b % 2 == 0:
+                nc.vector.tensor_scalar(staged[:], res[:, 0:PIECE], reader_sb[:, b : b + 1], None, ALU.mult)
+            else:
+                nc.scalar.activation(staged[:], res[:, 0:PIECE], ACT.Copy, scale=reader_sb[:, b : b + 1])
+            nc.sync.dma_start(out=out_view[:, b, PIECE:M], in_=staged[:])

@@ -114,8 +114,8 @@ def tile_list_framework_uptake_screen_kernel(
 
         def round_w1(a, u, on_vector):
             dst = tile("w1b%d_%d" % (a, u), [P, 2 * P * PACK], BF16)
-            dst_view = dst[:].rearrange("p (t m i) -> p m i t", t=2, i=PACK)
-            src_view = w1_sb[a][:].rearrange("p i (m t) -> p m i t", t=PACK)[:, :, :, 2 * u : 2 * u + 2]
+            dst_view = dst[:].rearrange("p (t m i) -> p m t i", t=2, i=PACK)
+            src_view = w1_sb[a][:].rearrange("p i (m t) -> p m t i", t=PACK)[:, :, 2 * u : 2 * u + 2, :]
             if on_vector:
                 nc.vector.tensor_copy(dst_view, src_view)
             else:
@@ -212,13 +212,13 @@ def tile_list_framework_uptake_screen_kernel(
 
         yq = []
         for j in range(PIECES):
+            prod = tile("prod%d" % j, [P, PACK, PIECE], F32)
+            for t in range(PACK):
+                nc.vector.tensor_tensor(
+                    prod[:, t, :], weighted[:, t, j * PIECE : (j + 1) * PIECE], thresh[j][:, t, :], ALU.mult
+                )
             y = tile("y%d" % j, [P, PIECE * PACK], BF16, tag="y")
-            nc.vector.tensor_tensor(
-                y[:].rearrange("p (g i t) -> p g t i", i=4, t=PACK),
-                weighted[:, :, j * PIECE : (j + 1) * PIECE].rearrange("p t (g i) -> p g t i", i=4),
-                thresh[j][:].rearrange("p t (g i) -> p g t i", i=4),
-                ALU.mult,
-            )
+            nc.vector.tensor_copy(y[:].rearrange("p (m t) -> p m t", t=PACK), prod[:].rearrange("p t m -> p m t"))
             yq.append(quantize("yq%d" % j, y, PIECE))
 
         out_view = out.rearrange("(b p) m -> p b m", p=P)

@@ -1,3 +1,4 @@
+import math
 from contextlib import ExitStack
 
 import concourse.mybir as mybir
@@ -19,12 +20,17 @@ ALU = mybir.AluOpType
 P = 128
 PACK = 4
 PASSES = K // (P * PACK)
+LAST = PASSES - 1
+QUADS = 4
+QUAD_ROWS = 4
+PER_COLUMN = 16
+BANKS = 8
 BANK = 512
 HALVES = S // BANK
-PIECE = 256
-PIECES = M // PIECE
+HALF_BANK = BANK // 2
+PIECE = M // 2
 BLOCKS = N // P
-QUADS = 4
+LINE = 4
 
 
 def tile_list_framework_uptake_screen_kernel(
@@ -32,18 +38,21 @@ def tile_list_framework_uptake_screen_kernel(
 ):
     nc = tc.nc
     with ExitStack() as ctx:
-        sb = ctx.enter_context(tc.tile_pool(name="sb", bufs=1))
+        sbuf = ctx.enter_context(tc.tile_pool(name="sbuf", bufs=1))
         psum = ctx.enter_context(tc.psum_pool(name="psum", bufs=1))
 
         def tile(name, shape, dtype, tag=None):
-            return sb.tile(shape, dtype, name=name, tag=tag or name, align_bytes=64)
+            return sbuf.tile(shape, dtype, name=name, tag=tag or name, align_bytes=64)
 
         def bank(index):
             return psum.tile([P, BANK], F32, name="bank%d" % index, tag="bank%d" % index)
 
-        offs_sb = tile("offs_sb", [P, S // 16], U16)
-        pos1_sb = tile("pos1_sb", [P, M // 16], U16)
-        pos2_sb = tile("pos2_sb", [P, M // 16], U16)
+        def entries(list_tile, first, count):
+            return list_tile[:, first // PER_COLUMN : (first + count) // PER_COLUMN]
+
+        offs_sb = tile("offs_sb", [P, S // PER_COLUMN], U16)
+        pos1_sb = tile("pos1_sb", [P, M // PER_COLUMN], U16)
+        pos2_sb = tile("pos2_sb", [P, M // PER_COLUMN], U16)
         tab_sb = [tile("tab%d" % a, [P, T], I32) for a in range(PASSES)]
         w1_sb = [tile("w1_%d" % a, [P, PACK, H], F32) for a in range(PASSES)]
         tab_planes = tile("tab_planes", [P, T], U8)
@@ -56,175 +65,195 @@ def tile_list_framework_uptake_screen_kernel(
         thr_sb = tile("thr_sb", [P, PACK], F32)
         reader_sb = tile("reader_sb", [P, BLOCKS], F32)
 
-        nc.gpsimd.memset(tab_planes[:].bitcast(I32), 0)
+        nc.vector.memset(tab_planes[:].bitcast(I32), 0)
         nc.vector.memset(w4_plane[:].bitcast(I32), 0)
-        for q in range(QUADS):
-            nc.scalar.dma_start(
-                out=tab_planes[32 * q : 32 * q + 4 * PASSES, :].bitcast(I32),
-                in_=tab_scales[:, 4 * q : 4 * q + 4, :].bitcast(I32),
-            )
 
         def load_tab(a):
             nc.sync.dma_start(out=tab_sb[a][:], in_=tab_words[a].rearrange("p n i -> p (n i)").bitcast(I32))
 
         def load_w1(a):
             rows = w1[a * P * PACK : (a + 1) * P * PACK, :]
-            nc.sync.dma_start(out=w1_sb[a][:], in_=rows.rearrange("(p i) c -> p i c", i=PACK))
+            nc.sync.dma_start(out=w1_sb[a][:], in_=rows.rearrange("(p i) r -> p i r", i=PACK))
 
-        def load_rows(dst, vec):
+        def load_by_slice(dst, vec):
             nc.sync.dma_start(out=dst[:], in_=vec.rearrange("(p t) -> p t", t=PACK))
 
         load_tab(0)
         nc.sync.dma_start(offs_sb[:], offs)
         load_w1(0)
-        load_rows(phase_sb, phase)
+        for q in range(QUADS):
+            nc.sync.dma_start(
+                out=tab_planes[32 * q : 32 * q + QUAD_ROWS * PASSES, :].bitcast(I32),
+                in_=tab_scales[:, QUAD_ROWS * q : QUAD_ROWS * (q + 1), :].bitcast(I32),
+            )
         load_tab(1)
+        load_by_slice(phase_sb, phase)
         load_w1(1)
-        load_w1(2)
-        load_tab(2)
+        load_w1(LAST)
+        load_tab(LAST)
         nc.sync.dma_start(pos1_sb[:], pos1)
-        load_rows(cal_sb, cal)
-        load_rows(calb_sb, calb)
+        load_by_slice(cal_sb, cal)
+        load_by_slice(calb_sb, calb)
         nc.sync.dma_start(out=pairs_sb[:], in_=pairs.rearrange("(p t) m -> p t m", t=PACK))
         nc.sync.dma_start(pos2_sb[:], pos2)
-        load_rows(thr_sb, thr)
+        load_by_slice(thr_sb, thr)
         nc.sync.dma_start(out=w4_sb[:].bitcast(I32), in_=w4_words[0].bitcast(I32))
         for q in range(QUADS):
             nc.sync.dma_start(
-                out=w4_plane[32 * q : 32 * q + 4, :].bitcast(I32),
-                in_=w4_scales[0, 4 * q : 4 * q + 4, :].bitcast(I32),
+                out=w4_plane[32 * q : 32 * q + QUAD_ROWS, :].bitcast(I32),
+                in_=w4_scales[0, QUAD_ROWS * q : QUAD_ROWS * (q + 1), :].bitcast(I32),
             )
         with nc.allow_non_contiguous_dma(reason="one value of reader for each output row"):
             nc.sync.dma_start(out=reader_sb[:], in_=reader.rearrange("(b p) -> p b", p=P))
 
-        sin_bias = tile("sin_bias", [P, PACK], F32)
-        nc.vector.tensor_scalar(sin_bias[:], phase_sb[:], -1.0 / 3.0, None, ALU.mult)
-
-        cols = BANK // 16
-
-        def gather_words(a, hf):
-            got = tile("v%d_%d" % (a, hf), [P, BANK], U32)
-            nc.vector.tensor_copy(got[:], tab_sb[a][:].bitcast(U32).indirect(offs_sb[:, hf * cols : (hf + 1) * cols]))
+        def gather_words(a, half, width):
+            got = tile("words%d_%d" % (a, half), [P, BANK], U32)
+            for lo in range(0, BANK, width):
+                picks = entries(offs_sb, half * BANK + lo, width)
+                nc.vector.tensor_copy(got[:, lo : lo + width], tab_sb[a][:].bitcast(U32).indirect(picks))
             return got
 
-        def gather_planes(hf):
-            got = tile("vs%d" % hf, [P, BANK], U8)
-            nc.vector.tensor_copy(got[:], tab_planes[:].indirect(offs_sb[:, hf * cols : (hf + 1) * cols]))
+        def gather_planes(half):
+            got = tile("planes%d" % half, [P, BANK], U8)
+            nc.vector.tensor_copy(got[:], tab_planes[:].indirect(entries(offs_sb, half * BANK, BANK)))
             return got
 
-        def round_w1(a, u, on_vector):
-            dst = tile("w1b%d_%d" % (a, u), [P, 2 * P * PACK], BF16)
-            dst_view = dst[:].rearrange("p (t m i) -> p m t i", t=2, i=PACK)
-            src_view = w1_sb[a][:].rearrange("p i (m t) -> p m t i", t=PACK)[:, :, 2 * u : 2 * u + 2, :]
-            if on_vector:
-                nc.vector.tensor_copy(dst_view, src_view)
-            else:
-                nc.scalar.copy(dst_view, src_view)
-            return dst
+        def round_w1(a, u, copy):
+            rounded = tile("w1_bf16_%d_%d" % (a, u), [P, 2 * P * PACK], BF16)
+            source = w1_sb[a][:].rearrange("p i (c t) -> p c i t", t=PACK)[:, :, :, 2 * u : 2 * u + 2]
+            copy(rounded[:].rearrange("p (e c i) -> p c i e", e=2, i=PACK), source)
+            return rounded
 
-        def quantize(name, src, width):
+        def quantize(name, rounded, width):
             codes = tile(name + "_codes", [P, width], U32)
             plane = tile(name + "_plane", [P, width], U8)
-            nc.vector.quantize_mx(out=codes[:].bitcast(FP8X4), scales=plane[:], in_=src[:])
+            nc.vector.quantize_mx(out=codes[:].bitcast(FP8X4), scales=plane[:], in_=rounded[:])
             return codes, plane
 
-        v = {}
-        wq = {}
-        v[0, 0] = gather_words(0, 0)
-        v[0, 1] = gather_words(0, 1)
-        vs = [gather_planes(hf) for hf in range(HALVES)]
-        wb0 = [round_w1(0, u, False) for u in range(2)]
-        v[1, 0] = gather_words(1, 0)
+        words = {}
+        w1_mx = {}
+        for half in range(HALVES):
+            words[0, half] = gather_words(0, half, BANK)
+        planes = [gather_planes(half) for half in range(HALVES)]
+        rounded_first = [round_w1(0, u, nc.scalar.copy) for u in range(2)]
+        words[1, 0] = gather_words(1, 0, BANK)
         for u in range(2):
-            wq[0, u] = quantize("w1q0_%d" % u, wb0[u], 2 * P)
-        v[1, 1] = gather_words(1, 1)
-        for a in (1, 2):
-            wb = [round_w1(a, 0, True), round_w1(a, 1, False)]
+            w1_mx[0, u] = quantize("w1_mx0_%d" % u, rounded_first[u], 2 * P)
+        words[1, 1] = gather_words(1, 1, BANK)
+        for a in range(1, PASSES):
+            first_copy = nc.vector.tensor_copy if a == LAST else nc.scalar.copy
+            rounded_pairs = [round_w1(a, 0, first_copy), round_w1(a, 1, nc.scalar.copy)]
             for u in range(2):
-                wq[a, u] = quantize("w1q%d_%d" % (a, u), wb[u], 2 * P)
-        v[2, 0] = gather_words(2, 0)
-        v[2, 1] = gather_words(2, 1)
+                w1_mx[a, u] = quantize("w1_mx%d_%d" % (a, u), rounded_pairs[u], 2 * P)
 
-        acc = {(t, hf): bank(HALVES * t + hf) for t in range(PACK) for hf in range(HALVES)}
+        half_sign = tile("half_sign", [P, PACK], F32)
+        half_phase = tile("half_phase", [P, PACK], F32)
+        sin_bias = tile("sin_bias", [P, PACK], F32)
+        slope = tile("slope", [P, PACK], F32)
+        nc.vector.tensor_scalar(half_sign[:], phase_sb[:], 0.0, -0.5, ALU.is_ge, ALU.add)
+        nc.vector.tensor_tensor(half_phase[:], phase_sb[:], half_sign[:], ALU.mult)
+        nc.vector.tensor_scalar(slope[:], half_sign[:], -4.0, None, ALU.mult)
+        nc.vector.tensor_scalar(sin_bias[:], half_phase[:], -math.pi / 4.0, None, ALU.add)
+
+        words[LAST, 0] = gather_words(LAST, 0, HALF_BANK)
+        words[LAST, 1] = gather_words(LAST, 1, BANK)
+
+        whole_banks = [(2, 0), (0, 1), (1, 1), (3, 0), (2, 1), (3, 1)]
+        sums = [[(0, lo, HALF_BANK), (1, lo, HALF_BANK)] for lo in (0, HALF_BANK)]
+        sums += [[(t, half * BANK, BANK)] for t, half in whole_banks]
+        acc = [bank(index) for index in range(BANKS)]
         for a in range(PASSES):
-            for hf in range(HALVES):
-                for t in range(PACK):
-                    codes, plane = wq[a, t // 2]
-                    lo = (t % 2) * P
+            for index, members in enumerate(sums):
+                for place, (t, first, width) in enumerate(members):
+                    codes, plane = w1_mx[a, t // 2]
+                    stationary = slice((t % 2) * P, (t % 2 + 1) * P)
+                    half, inner = divmod(first, BANK)
                     nc.tensor.matmul_mx(
-                        out=acc[t, hf][:],
-                        lhsT=codes[:, lo : lo + P].bitcast(FP8X4),
-                        lhsT_scale=plane[:, lo : lo + P],
-                        rhs=v[a, hf][:].bitcast(FP8X4),
-                        rhs_scale=vs[hf][4 * a : P, :],
-                        start=(a == 0),
-                        stop=(a == PASSES - 1),
+                        out=acc[index][:, place * width : (place + 1) * width],
+                        lhsT=codes[:, stationary].bitcast(FP8X4),
+                        lhsT_scale=plane[:, stationary],
+                        rhs=words[a, half][:, inner : inner + width].bitcast(FP8X4),
+                        rhs_scale=planes[half][QUAD_ROWS * a : P, inner : inner + width],
+                        start=(a == 0 and place == 0),
+                        stop=(a == LAST and place == len(members) - 1),
                     )
 
-        order = [(0, 0), (1, 0), (0, 1), (1, 1), (2, 0), (2, 1), (3, 0), (3, 1)]
         h = [tile("h%d" % t, [P, S], F32) for t in range(PACK)]
-        third = [tile("third%d" % t, [P, S], F32) for t in range(PACK)]
-        s = {}
-        for t, hf in order:
-            s[t, hf] = third[t][:, hf * BANK : (hf + 1) * BANK]
-            nc.scalar.activation(s[t, hf], acc[t, hf][:], ACT.Sin, bias=sin_bias[:, t : t + 1], scale=-1.0 / 3.0)
-        sq = {}
-        for first in range(0, len(order), 2):
-            both = order[first : first + 2]
-            for t, hf in both:
-                sq[t, hf] = tile("sq%d_%d" % (t, hf), [P, BANK], F32)
-                nc.vector.scalar_tensor_tensor(sq[t, hf][:], s[t, hf], 4.0, s[t, hf], ALU.mult, ALU.mult)
-            for t, hf in both:
-                nc.vector.scalar_tensor_tensor(
-                    h[t][:, hf * BANK : (hf + 1) * BANK], sq[t, hf][:], 3.0, s[t, hf], ALU.subtract, ALU.mult
+        sine = [tile("sine%d" % t, [P, S], F32) for t in range(PACK)]
+        for index, members in enumerate(sums):
+            for place, (t, first, width) in enumerate(members):
+                nc.scalar.activation(
+                    sine[t][:, first : first + width],
+                    acc[index][:, place * width : (place + 1) * width],
+                    ACT.Sin,
+                    bias=sin_bias[:, t : t + 1],
+                    scale=half_sign[:, t : t + 1],
+                )
+        square = [tile("square%d" % t, [P, S], F32) for t in range(PACK)]
+        sine_order = [(0, 0), (1, 0)] + whole_banks
+        for step in range(0, len(sine_order), 2):
+            both = [(t, slice(half * BANK, (half + 1) * BANK)) for t, half in sine_order[step : step + 2]]
+            for t, cols in both:
+                nc.vector.tensor_tensor(square[t][:, cols], sine[t][:, cols], sine[t][:, cols], ALU.mult)
+            for t, cols in both:
+                nc.vector.tensor_scalar(
+                    h[t][:, cols], square[t][:, cols], 0.5, slope[:, t : t + 1], ALU.subtract, ALU.mult
                 )
 
-        gate = [tile("gate%d" % t, [P, M], F32) for t in range(PACK)]
-        pcols = PIECE // 16
-        thresh = [
-            tile("thresh0", [P, PACK, PIECE], F32),
-            tile("thresh1", [P, PACK, PIECE], F32, tag="third%d" % (PACK - 1)),
+        looked = [
+            tile("looked0", [P, 2, PACK, PIECE], F32),
+            tile("looked1", [P, 2, PACK, PIECE], F32, tag="square%d" % (PACK - 1)),
         ]
+        gate = [results[:, 0] for results in looked]
+        thresh = [results[:, 1] for results in looked]
+
+        def look_gate(j, t):
+            nc.scalar.activation(
+                gate[j][:, t, :],
+                h[t][:].indirect(entries(pos1_sb, j * PIECE, PIECE)),
+                ACT.Sigmoid,
+                bias=calb_sb[:, t : t + 1],
+                scale=cal_sb[:, t : t + 1],
+            )
 
         def look_thresh(j, t):
             nc.scalar.activation(
                 thresh[j][:, t, :],
-                h[t][:].indirect(pos2_sb[:, j * pcols : (j + 1) * pcols]),
+                h[t][:].indirect(entries(pos2_sb, j * PIECE, PIECE)),
                 ACT.Sigmoid,
                 bias=thr_sb[:, t : t + 1],
             )
 
         for t in range(PACK):
-            nc.scalar.activation(
-                gate[t][:],
-                h[t][:].indirect(pos1_sb[:]),
-                ACT.Sigmoid,
-                bias=calb_sb[:, t : t + 1],
-                scale=cal_sb[:, t : t + 1],
-            )
+            look_gate(0, t)
             look_thresh(0, t)
+        for t in range(PACK):
+            look_gate(1, t)
         for t in range(PACK):
             look_thresh(1, t)
 
-        weighted = tile("weighted", [P, PACK, M], F32)
-        for t in range(PACK):
-            nc.vector.tensor_tensor(weighted[:, t, :], gate[t][:], pairs_sb[:, t, :], ALU.mult)
+        weighted = [tile("weighted%d" % j, [P, PACK, PIECE], F32) for j in range(2)]
 
-        yq = []
-        for j in range(PIECES):
-            prod = tile("prod%d" % j, [P, PACK, PIECE], F32)
-            for t in range(PACK):
-                nc.vector.tensor_tensor(
-                    prod[:, t, :], weighted[:, t, j * PIECE : (j + 1) * PIECE], thresh[j][:, t, :], ALU.mult
-                )
+        def weigh(j, slices):
+            nc.vector.tensor_tensor(
+                weighted[j][:, slices, :],
+                gate[j][:, slices, :],
+                pairs_sb[:, slices, j * PIECE : (j + 1) * PIECE],
+                ALU.mult,
+            )
+
+        def quantize_y(j):
             y = tile("y%d" % j, [P, PIECE * PACK], BF16, tag="y")
-            nc.vector.tensor_copy(y[:].rearrange("p (m t) -> p m t", t=PACK), prod[:].rearrange("p t m -> p m t"))
-            yq.append(quantize("yq%d" % j, y, PIECE))
+            nc.vector.tensor_tensor(
+                y[:].rearrange("p (g i t) -> p g t i", i=LINE, t=PACK),
+                weighted[j][:].rearrange("p t (g i) -> p g t i", i=LINE),
+                thresh[j].rearrange("p t (g i) -> p g t i", i=LINE),
+                ALU.mult,
+            )
+            return quantize("y_mx%d" % j, y, PIECE)
 
-        out_view = out.rearrange("(b p) m -> p b m", p=P)
-
-        def second(j, b, dst):
-            codes, plane = yq[j]
+        def multiply_w4(y_mx, b, dst):
+            codes, plane = y_mx
             nc.tensor.matmul_mx(
                 out=dst,
                 lhsT=w4_sb[:, 2 * P * b : 2 * P * (b + 1)].bitcast(FP4X4),
@@ -235,23 +264,35 @@ def tile_list_framework_uptake_screen_kernel(
                 stop=True,
             )
 
+        out_view = out.rearrange("(b p) m -> p b m", p=P)
+
+        weigh(0, slice(0, PACK - 1))
+        weigh(0, slice(PACK - 1, PACK))
+        y_first = quantize_y(0)
         for pair in range(BLOCKS // 2):
-            res = bank(pair)
-            staged = tile("first%d" % pair, [P, 2, PIECE], F32)
-            for i in range(2):
-                second(0, 2 * pair + i, res[:, i * PIECE : (i + 1) * PIECE])
-            for i in range(2):
-                b = 2 * pair + i
-                nc.scalar.activation(
-                    staged[:, i, :], res[:, i * PIECE : (i + 1) * PIECE], ACT.Copy, scale=reader_sb[:, b : b + 1]
-                )
-            nc.sync.dma_start(out=out_view[:, 2 * pair : 2 * pair + 2, 0:PIECE], in_=staged[:])
+            blocks = slice(2 * pair, 2 * pair + 2)
+            result = bank(pair)
+            staged = tile("staged_first%d" % pair, [P, 2, PIECE], F32)
+            for e in range(2):
+                multiply_w4(y_first, 2 * pair + e, result[:, e * PIECE : (e + 1) * PIECE])
+            if pair == 0:
+                weigh(1, slice(0, PACK // 2))
+            nc.vector.tensor_tensor(
+                staged[:],
+                result[:].rearrange("p (e m) -> p e m", e=2),
+                reader_sb[:, blocks].unsqueeze(2).to_broadcast([P, 2, PIECE]),
+                ALU.mult,
+            )
+            nc.sync.dma_start(out=out_view[:, blocks, 0:PIECE], in_=staged[:])
+
+        weigh(1, slice(PACK // 2, PACK))
+        y_second = quantize_y(1)
         for b in range(BLOCKS):
-            res = bank((BLOCKS // 2 + b) % 8)
-            staged = tile("last%d" % b, [P, PIECE], F32)
-            second(1, b, res[:, 0:PIECE])
-            if b % 2 == 0:
-                nc.vector.tensor_scalar(staged[:], res[:, 0:PIECE], reader_sb[:, b : b + 1], None, ALU.mult)
+            result = bank((BLOCKS // 2 + b) % BANKS)
+            staged = tile("staged_second%d" % b, [P, PIECE], F32)
+            multiply_w4(y_second, b, result[:, 0:PIECE])
+            if b % 2 == 1:
+                nc.vector.tensor_scalar(staged[:], result[:, 0:PIECE], reader_sb[:, b : b + 1], None, ALU.mult)
             else:
-                nc.scalar.activation(staged[:], res[:, 0:PIECE], ACT.Copy, scale=reader_sb[:, b : b + 1])
+                nc.scalar.activation(staged[:], result[:, 0:PIECE], ACT.Copy, scale=reader_sb[:, b : b + 1])
             nc.sync.dma_start(out=out_view[:, b, PIECE:M], in_=staged[:])

import math
from contextlib import ExitStack

import concourse.mybir as mybir

K, T, S, M, H, N = 1536, 2048, 1024, 512, 512, 768
FLOPS = 2 * K * H * S + 2 * H * N * M

F32 = mybir.dt.float32
BF16 = mybir.dt.bfloat16
I32 = mybir.dt.int32
U32 = mybir.dt.uint32
U16 = mybir.dt.uint16
U8 = mybir.dt.uint8
FP8X4 = mybir.dt.float8_e4m3fn_x4
FP4X4 = mybir.dt.float4_e2m1fn_x4
ACT = mybir.ActivationFunctionType
ALU = mybir.AluOpType

P = 128
PACK = 4
PASSES = K // (P * PACK)
LAST = PASSES - 1
QUADS = 4
QUAD_ROWS = 4
PER_COLUMN = 16
BANKS = 8
BANK = 512
HALVES = S // BANK
HALF_BANK = BANK // 2
PIECE = M // 2
BLOCKS = N // P
LINE = 4


def tile_list_framework_uptake_screen_kernel(
    tc, tab_words, tab_scales, offs, pos1, pos2, w1, phase, cal, calb, thr, pairs, w4_words, w4_scales, reader, out
):
    nc = tc.nc
    with ExitStack() as ctx:
        sbuf = ctx.enter_context(tc.tile_pool(name="sbuf", bufs=1))
        psum = ctx.enter_context(tc.psum_pool(name="psum", bufs=1))

        def tile(name, shape, dtype, tag=None):
            return sbuf.tile(shape, dtype, name=name, tag=tag or name, align_bytes=64)

        def bank(index):
            return psum.tile([P, BANK], F32, name="bank%d" % index, tag="bank%d" % index)

        def entries(list_tile, first, count):
            return list_tile[:, first // PER_COLUMN : (first + count) // PER_COLUMN]

        offs_sb = tile("offs_sb", [P, S // PER_COLUMN], U16)
        pos1_sb = tile("pos1_sb", [P, M // PER_COLUMN], U16)
        pos2_sb = tile("pos2_sb", [P, M // PER_COLUMN], U16)
        tab_sb = [tile("tab%d" % a, [P, T], I32) for a in range(PASSES)]
        w1_sb = [tile("w1_%d" % a, [P, PACK, H], F32) for a in range(PASSES)]
        tab_planes = tile("tab_planes", [P, T], U8)
        w4_plane = tile("w4_plane", [P, N], U8)
        w4_sb = tile("w4_sb", [P, 2 * N], U8)
        pairs_sb = tile("pairs_sb", [P, PACK, M], F32)
        phase_sb = tile("phase_sb", [P, PACK], F32)
        cal_sb = tile("cal_sb", [P, PACK], F32)
        calb_sb = tile("calb_sb", [P, PACK], F32)
        thr_sb = tile("thr_sb", [P, PACK], F32)
        reader_sb = tile("reader_sb", [P, BLOCKS], F32)

        nc.vector.memset(tab_planes[:].bitcast(I32), 0)
        nc.vector.memset(w4_plane[:].bitcast(I32), 0)

        def load_tab(a):
            nc.sync.dma_start(out=tab_sb[a][:], in_=tab_words[a].rearrange("p n i -> p (n i)").bitcast(I32))

        def load_w1(a):
            rows = w1[a * P * PACK : (a + 1) * P * PACK, :]
            nc.sync.dma_start(out=w1_sb[a][:], in_=rows.rearrange("(p i) r -> p i r", i=PACK))

        def load_by_slice(dst, vec):
            nc.sync.dma_start(out=dst[:], in_=vec.rearrange("(p t) -> p t", t=PACK))

        load_tab(0)
        nc.sync.dma_start(offs_sb[:], offs)
        load_w1(0)
        for q in range(QUADS):
            nc.sync.dma_start(
                out=tab_planes[32 * q : 32 * q + QUAD_ROWS * PASSES, :].bitcast(I32),
                in_=tab_scales[:, QUAD_ROWS * q : QUAD_ROWS * (q + 1), :].bitcast(I32),
            )
        load_tab(1)
        load_by_slice(phase_sb, phase)
        load_w1(1)
        load_w1(LAST)
        load_tab(LAST)
        nc.sync.dma_start(pos1_sb[:], pos1)
        load_by_slice(cal_sb, cal)
        load_by_slice(calb_sb, calb)
        nc.sync.dma_start(out=pairs_sb[:], in_=pairs.rearrange("(p t) m -> p t m", t=PACK))
        nc.sync.dma_start(pos2_sb[:], pos2)
        load_by_slice(thr_sb, thr)
        nc.sync.dma_start(out=w4_sb[:].bitcast(I32), in_=w4_words[0].bitcast(I32))
        for q in range(QUADS):
            nc.sync.dma_start(
                out=w4_plane[32 * q : 32 * q + QUAD_ROWS, :].bitcast(I32),
                in_=w4_scales[0, QUAD_ROWS * q : QUAD_ROWS * (q + 1), :].bitcast(I32),
            )
        with nc.allow_non_contiguous_dma(reason="one value of reader for each output row"):
            nc.sync.dma_start(out=reader_sb[:], in_=reader.rearrange("(b p) -> p b", p=P))

        def gather_words(a, half, width):
            got = tile("words%d_%d" % (a, half), [P, BANK], U32)
            for lo in range(0, BANK, width):
                picks = entries(offs_sb, half * BANK + lo, width)
                nc.vector.tensor_copy(got[:, lo : lo + width], tab_sb[a][:].bitcast(U32).indirect(picks))
            return got

        def gather_planes(half):
            got = tile("planes%d" % half, [P, BANK], U8)
            nc.vector.tensor_copy(got[:], tab_planes[:].indirect(entries(offs_sb, half * BANK, BANK)))
            return got

        def round_w1(a, u, copy):
            rounded = tile("w1_bf16_%d_%d" % (a, u), [P, 2 * P * PACK], BF16)
            source = w1_sb[a][:].rearrange("p i (c t) -> p c i t", t=PACK)[:, :, :, 2 * u : 2 * u + 2]
            copy(rounded[:].rearrange("p (e c i) -> p c i e", e=2, i=PACK), source)
            return rounded

        def quantize(name, rounded, width):
            codes = tile(name + "_codes", [P, width], U32)
            plane = tile(name + "_plane", [P, width], U8)
            nc.vector.quantize_mx(out=codes[:].bitcast(FP8X4), scales=plane[:], in_=rounded[:])
            return codes, plane

        words = {}
        w1_mx = {}
        for half in range(HALVES):
            words[0, half] = gather_words(0, half, BANK)
        planes = [gather_planes(half) for half in range(HALVES)]
        rounded_first = [round_w1(0, u, nc.scalar.copy) for u in range(2)]
        words[1, 0] = gather_words(1, 0, BANK)
        for u in range(2):
            w1_mx[0, u] = quantize("w1_mx0_%d" % u, rounded_first[u], 2 * P)
        words[1, 1] = gather_words(1, 1, BANK)
        for a in range(1, PASSES):
            first_copy = nc.vector.tensor_copy if a == LAST else nc.scalar.copy
            rounded_pairs = [round_w1(a, 0, first_copy), round_w1(a, 1, nc.scalar.copy)]
            for u in range(2):
                w1_mx[a, u] = quantize("w1_mx%d_%d" % (a, u), rounded_pairs[u], 2 * P)

        half_sign = tile("half_sign", [P, PACK], F32)
        half_phase = tile("half_phase", [P, PACK], F32)
        sin_bias = tile("sin_bias", [P, PACK], F32)
        slope = tile("slope", [P, PACK], F32)
        nc.vector.tensor_scalar(half_sign[:], phase_sb[:], 0.0, -0.5, ALU.is_ge, ALU.add)
        nc.vector.tensor_tensor(half_phase[:], phase_sb[:], half_sign[:], ALU.mult)
        nc.vector.tensor_scalar(slope[:], half_sign[:], -4.0, None, ALU.mult)
        nc.vector.tensor_scalar(sin_bias[:], half_phase[:], -math.pi / 4.0, None, ALU.add)

        words[LAST, 0] = gather_words(LAST, 0, HALF_BANK)
        words[LAST, 1] = gather_words(LAST, 1, BANK)

        whole_banks = [(2, 0), (0, 1), (1, 1), (3, 0), (2, 1), (3, 1)]
        sums = [[(0, lo, HALF_BANK), (1, lo, HALF_BANK)] for lo in (0, HALF_BANK)]
        sums += [[(t, half * BANK, BANK)] for t, half in whole_banks]
        acc = [bank(index) for index in range(BANKS)]
        for a in range(PASSES):
            for index, members in enumerate(sums):
                for place, (t, first, width) in enumerate(members):
                    codes, plane = w1_mx[a, t // 2]
                    stationary = slice((t % 2) * P, (t % 2 + 1) * P)
                    half, inner = divmod(first, BANK)
                    nc.tensor.matmul_mx(
                        out=acc[index][:, place * width : (place + 1) * width],
                        lhsT=codes[:, stationary].bitcast(FP8X4),
                        lhsT_scale=plane[:, stationary],
                        rhs=words[a, half][:, inner : inner + width].bitcast(FP8X4),
                        rhs_scale=planes[half][QUAD_ROWS * a : P, inner : inner + width],
                        start=(a == 0 and place == 0),
                        stop=(a == LAST and place == len(members) - 1),
                    )

        h = [tile("h%d" % t, [P, S], F32) for t in range(PACK)]
        sine = [tile("sine%d" % t, [P, S], F32) for t in range(PACK)]
        for index, members in enumerate(sums):
            for place, (t, first, width) in enumerate(members):
                nc.scalar.activation(
                    sine[t][:, first : first + width],
                    acc[index][:, place * width : (place + 1) * width],
                    ACT.Sin,
                    bias=sin_bias[:, t : t + 1],
                    scale=half_sign[:, t : t + 1],
                )
        square = [tile("square%d" % t, [P, S], F32) for t in range(PACK)]
        sine_order = [(0, 0), (1, 0)] + whole_banks
        for step in range(0, len(sine_order), 2):
            both = [(t, slice(half * BANK, (half + 1) * BANK)) for t, half in sine_order[step : step + 2]]
            for t, cols in both:
                nc.vector.tensor_tensor(square[t][:, cols], sine[t][:, cols], sine[t][:, cols], ALU.mult)
            for t, cols in both:
                nc.vector.tensor_scalar(
                    h[t][:, cols], square[t][:, cols], 0.5, slope[:, t : t + 1], ALU.subtract, ALU.mult
                )

        looked = [
            tile("looked0", [P, 2, PACK, PIECE], F32),
            tile("looked1", [P, 2, PACK, PIECE], F32, tag="square%d" % (PACK - 1)),
        ]
        gate = [results[:, 0] for results in looked]
        thresh = [results[:, 1] for results in looked]

        def look_gate(j, t):
            nc.scalar.activation(
                gate[j][:, t, :],
                h[t][:].indirect(entries(pos1_sb, j * PIECE, PIECE)),
                ACT.Sigmoid,
                bias=calb_sb[:, t : t + 1],
                scale=cal_sb[:, t : t + 1],
            )

        def look_thresh(j, t):
            nc.scalar.activation(
                thresh[j][:, t, :],
                h[t][:].indirect(entries(pos2_sb, j * PIECE, PIECE)),
                ACT.Sigmoid,
                bias=thr_sb[:, t : t + 1],
            )

        for t in range(PACK):
            look_gate(0, t)
            look_thresh(0, t)
        for t in range(PACK):
            look_gate(1, t)
        for t in range(PACK):
            look_thresh(1, t)

        weighted = [tile("weighted%d" % j, [P, PACK, PIECE], F32) for j in range(2)]

        def weigh(j, slices):
            nc.vector.tensor_tensor(
                weighted[j][:, slices, :],
                gate[j][:, slices, :],
                pairs_sb[:, slices, j * PIECE : (j + 1) * PIECE],
                ALU.mult,
            )

        def quantize_y(j):
            y = tile("y%d" % j, [P, PIECE * PACK], BF16, tag="y")
            nc.vector.tensor_tensor(
                y[:].rearrange("p (g i t) -> p g t i", i=LINE, t=PACK),
                weighted[j][:].rearrange("p t (g i) -> p g t i", i=LINE),
                thresh[j].rearrange("p t (g i) -> p g t i", i=LINE),
                ALU.mult,
            )
            return quantize("y_mx%d" % j, y, PIECE)

        def multiply_w4(y_mx, b, dst):
            codes, plane = y_mx
            nc.tensor.matmul_mx(
                out=dst,
                lhsT=w4_sb[:, 2 * P * b : 2 * P * (b + 1)].bitcast(FP4X4),
                lhsT_scale=w4_plane[:, P * b : P * (b + 1)],
                rhs=codes[:].bitcast(FP8X4),
                rhs_scale=plane[:],
                start=True,
                stop=True,
            )

        out_view = out.rearrange("(b p) m -> p b m", p=P)

        weigh(0, slice(0, PACK - 1))
        weigh(0, slice(PACK - 1, PACK))
        y_first = quantize_y(0)
        for pair in range(BLOCKS // 2):
            blocks = slice(2 * pair, 2 * pair + 2)
            result = bank(pair)
            staged = tile("staged_first%d" % pair, [P, 2, PIECE], F32)
            for e in range(2):
                multiply_w4(y_first, 2 * pair + e, result[:, e * PIECE : (e + 1) * PIECE])
            if pair == 0:
                weigh(1, slice(0, PACK // 2))
            nc.vector.tensor_tensor(
                staged[:],
                result[:].rearrange("p (e m) -> p e m", e=2),
                reader_sb[:, blocks].unsqueeze(2).to_broadcast([P, 2, PIECE]),
                ALU.mult,
            )
            nc.sync.dma_start(out=out_view[:, blocks, 0:PIECE], in_=staged[:])

        weigh(1, slice(PACK // 2, PACK))
        y_second = quantize_y(1)
        for b in range(BLOCKS):
            result = bank((BLOCKS // 2 + b) % BANKS)
            staged = tile("staged_second%d" % b, [P, PIECE], F32)
            multiply_w4(y_second, b, result[:, 0:PIECE])
            if b % 2 == 1:
                nc.vector.tensor_scalar(staged[:], result[:, 0:PIECE], reader_sb[:, b : b + 1], None, ALU.mult)
            else:
                nc.scalar.activation(staged[:], result[:, 0:PIECE], ACT.Copy, scale=reader_sb[:, b : b + 1])
            nc.sync.dma_start(out=out_view[:, b, PIECE:M], in_=staged[:])
